import numpy as np, ml_dtypes
CORES = [56,64,184,192,312,320,440,448]
N = 8
R = 64
def setup_inputs(rng):
    m = (rng.standard_normal((N, 128, 128), dtype=np.float32) / 11).astype(ml_dtypes.bfloat16)
    q = rng.standard_normal((128, R), dtype=np.float32).astype(ml_dtypes.bfloat16)
    return {"m": m, "mt": m.transpose(0, 2, 1).copy(), "q": np.broadcast_to(q, (N, 128, R)).copy()}
def setup_inputs_big(rng):
    d = setup_inputs(rng)
    for k in ("m", "mt", "q"): d[k] = (d[k].astype(np.float32) * 1024.0).astype(d[k].dtype)
    return d
def setup_inputs_small(rng):
    d = setup_inputs(rng)
    for k in ("m", "mt", "q"): d[k] = (d[k].astype(np.float32) * (1 / 1024.0)).astype(d[k].dtype)
    return d
def setup_inputs_apart(rng):
    d = setup_inputs(rng)
    f = (10.0 ** rng.permutation(np.linspace(-1.5, 1.5, N))).astype(np.float32).reshape(N, 1, 1)
    for k in ("m", "mt"): d[k] = (d[k].astype(np.float32) * f).astype(d[k].dtype)
    return d
def reference(m, mt, q):
    M, MT, Q = m.astype(np.float64), mt.astype(np.float64), q.astype(np.float64)
    p = sum(MT[j].T @ Q[j] for j in range(N))
    q2 = sum(M[j].T @ p for j in range(N))
    return {"p": np.broadcast_to(p.astype(ml_dtypes.bfloat16), (N, 128, R)), "q2": np.broadcast_to(q2.astype(ml_dtypes.bfloat16), (N, 128, R))}

@@ -1,0 +1,163 @@
+from concourse.bass import DstId, RemoteDMATransfer
+
+P = 128
+R = 64
+BF = "bfloat16"
+
+SCRATCH = {
+    "dm": ("dram", [P, P], BF),
+    "kd": ("dram", [2, P, P], BF),
+    "rd": ("dram", [P, P], BF),
+    "z": ("sbuf", [P, P + 1], BF),
+    "dz": ("dram", [P + 1, P], BF),
+    "w0": ("sbuf", [P, P], BF),
+    "w1": ("sbuf", [P, P], BF),
+    "w2": ("sbuf", [P, P], BF),
+    "w3": ("sbuf", [P, P], BF),
+    "w4": ("sbuf", [P, P], BF),
+    "qi": ("sbuf", [P, R + P], BF),
+    "ps": ("sbuf", [P, R + P], BF),
+    "o2": ("sbuf", [P, R], BF),
+    "acc": ("psum", [P, 512], "float32"),
+    "acc2": ("psum", [P, 512], "float32"),
+}
+SEMAPHORES = ["ld_dm", "ld_w0", "ld_q", "ld_w1", "st_p", "st_q2", "fill", "seed", "idn", "in1", "cab", "xa", "xb",
+              "sent", "mm1", "cp1", "mm2", "cp2"]
+
+
+def _engines(mask):
+    return [e for e in range(mask.bit_length()) if (mask >> e) & 1]
+
+
+def _bits(engines):
+    return sum(1 << e for e in engines)
+
+
+def _plan(T, topo):
+    ranks = list(T.cores)
+    n = topo.CORES_PER_CHIP
+    plan = {}
+    for r in ranks:
+        partner = [s for s in ranks if topo.same_plane(r, s)][0]
+        cabled = [s for s in ranks if topo.rack(topo.host(s)) != topo.rack(topo.host(r))
+                  and topo.chip(s) == topo.chip(r) and topo.may_write(r, s)][0]
+        cross = [s for s in ranks if s != r and topo.host(s) == topo.host(r)][0]
+        chip = [c for c in range(max(0, r - n), r + n + 1)
+                if topo.host(c) == topo.host(r) and topo.chip(c) == topo.chip(r)]
+        helper = [c for c in chip if c != r and topo.die(c) == topo.die(r) and topo.may_write(c, cross)][0]
+        plan[r] = {"partner": partner, "cabled": cabled, "cross": cross, "helper": helper}
+    return plan
+
+
+def _dst(topo, dst, src):
+    rid, pid = topo.addr(dst, src)
+    return DstId(rid=rid, pnc=pid)
+
+
+def _step1_engines(topo, plan, r):
+    mask = topo.mask(r, plan[plan[r]["partner"]]["helper"]) & topo.mask(r, plan[r]["helper"]) & topo.mask(r, plan[r]["partner"])
+    return _engines(mask)
+
+
+def _helper_program(g, core, T, topo, plan, r):
+    S = T.sem
+    near = plan[r]["cross"]
+    far = plan[plan[r]["cabled"]]["cross"]
+    eng = _engines(topo.mask(core, near) & topo.mask(core, far) & topo.mask(core, r))
+    half = len(eng) // 2
+
+    g.vector.memset(T.z[:, :], 0.0).then_inc(S.fill, 1)
+    g.vector.wait_ge(S.fill, 1)
+    g.vector.memset(T.z[:, 0:1], 1.0).then_inc(S.fill, 1)
+    g.sync.wait_ge(S.fill, 2)
+    g.sync.dma_start(T.dz[:, :], T.z[:, :]).then_inc(S.seed, 16)
+    g.wait_ge(S.seed, 16)
+    rid, pid = topo.addr(r, core)
+    g.remote_dma(out_ap=T.qi[:, R:R + P], in_ap=T.dz[0:P, :], remote_sem=S.idn, local_sem=S.sent,
+                 pid=pid, routing_id=rid, dma_engine_mask=_bits(eng))
+
+    g.wait_ge(S.in1, len(_step1_engines(topo, plan, r)) + len(_step1_engines(topo, plan, plan[r]["partner"])))
+    srcs = [T.kd[0], T.kd[1]]
+    g.remote_dma_fused([
+        RemoteDMATransfer(dst_ids=[_dst(topo, far, core)], dma_engine_mask=_bits(eng[:half]), remote_sem=S.xb,
+                          srcs=srcs, dsts=[T.w4[:, :]], alu_op=1),
+        RemoteDMATransfer(dst_ids=[_dst(topo, near, core)], dma_engine_mask=_bits(eng[half:]), remote_sem=S.xa,
+                          srcs=srcs, dsts=[T.w3[:, :]], alu_op=1),
+    ], local_sem=S.sent)
+    g.wait_ge(S.sent, 2 * len(eng))
+
+
+def _rank_program(g, core, T, topo, plan):
+    S = T.sem
+    me = plan[core]
+    partner, cabled = me["partner"], me["cabled"]
+
+    g.sync.dma_start(T.dm[:, :], T.mt[:, :]).then_inc(S.ld_dm, 16)
+    g.scalar.dma_start(T.qi[:, 0:R], T.q[:, :]).then_inc(S.ld_q, 16)
+    g.scalar.dma_start(T.w0[:, :], T.mt[:, :]).then_inc(S.ld_w0, 16)
+
+    eng1 = _step1_engines(topo, plan, core)
+    g.wait_ge(S.ld_dm, 16)
+    g.remote_dma_fused([
+        RemoteDMATransfer(dst_ids=[_dst(topo, plan[partner]["helper"], core), _dst(topo, me["helper"], core),
+                                   _dst(topo, partner, core)],
+                          dma_engine_mask=_bits(eng1), remote_sem=S.in1,
+                          srcs=[T.dm[:, :]], dsts=[T.kd[1], T.kd[0], T.rd[:, :]], alu_op=0),
+    ], local_sem=S.sent)
+
+    n_in = len(_step1_engines(topo, plan, partner))
+    eng2 = _engines(topo.mask(core, cabled))
+    g.wait_ge(S.in1, n_in)
+    g.remote_dma_fused([
+        RemoteDMATransfer(dst_ids=[_dst(topo, cabled, core)], dma_engine_mask=_bits(eng2), remote_sem=S.cab,
+                          srcs=[T.dm[:, :], T.rd[:, :]], dsts=[T.w2[:, :]], alu_op=1),
+    ], local_sem=S.sent)
+    g.sync.wait_ge(S.in1, n_in)
+    g.sync.dma_start(T.w1[:, :], T.rd[:, :]).then_inc(S.ld_w1, 16)
+
+    def helper_engines(r):
+        k = plan[r]["helper"]
+        return _engines(topo.mask(k, plan[r]["cross"]) & topo.mask(k, plan[plan[r]["cabled"]]["cross"]) & topo.mask(k, r))
+
+    n_idn = len(helper_engines(core))
+    n_xa = len(helper_engines(me["cross"])) - len(helper_engines(me["cross"])) // 2
+    n_xb = len(helper_engines(plan[cabled]["cross"])) // 2
+    n_cab = len(_engines(topo.mask(cabled, core)))
+    t, v = g.tensor, g.vector
+    out1 = T.acc[:, 0:R + P]
+    t.wait_ge(S.ld_q, 16)
+    t.wait_ge(S.idn, n_idn)
+    t.wait_ge(S.ld_w0, 16)
+    t.matmul(out1, T.w0[:, :], T.qi[:, :], True, False)
+    t.wait_ge(S.ld_w1, 16)
+    t.matmul(out1, T.w1[:, :], T.qi[:, :], False, False)
+    t.wait_ge(S.cab, n_cab)
+    t.matmul(out1, T.w2[:, :], T.qi[:, :], False, False)
+    t.wait_ge(S.xa, n_xa)
+    t.matmul(out1, T.w3[:, :], T.qi[:, :], False, False)
+    t.wait_ge(S.xb, n_xb)
+    t.matmul(out1, T.w4[:, :], T.qi[:, :], False, True).then_inc(S.mm1, 1)
+    v.wait_ge(S.mm1, 1)
+    v.tensor_copy(T.ps[:, :], out1).then_inc(S.cp1, 1)
+    g.scalar.wait_ge(S.cp1, 1)
+    g.scalar.dma_start(T.p[:, :], T.ps[:, 0:R]).then_inc(S.st_p, 16)
+    t.wait_ge(S.cp1, 1)
+    t.matmul(T.acc2[:, 0:R], T.ps[:, R:R + P], T.ps[:, 0:R], True, True).then_inc(S.mm2, 1)
+    v.wait_ge(S.mm2, 1)
+    v.tensor_copy(T.o2[:, :], T.acc2[:, 0:R]).then_inc(S.cp2, 1)
+    g.sync.wait_ge(S.cp2, 1)
+    g.sync.dma_start(T.q2[:, :], T.o2[:, :]).then_inc(S.st_q2, 16)
+
+    g.wait_ge(S.sent, len(eng1) + len(eng2))
+    g.scalar.wait_ge(S.st_p, 16)
+    g.sync.wait_ge(S.st_q2, 16)
+
+
+def rank_program(g, core, T, topo):
+    plan = _plan(T, topo)
+    if T.rank_of(core) is not None:
+        _rank_program(g, core, T, topo, plan)
+        return
+    for r in plan:
+        if plan[r]["helper"] == core:
+            _helper_program(g, core, T, topo, plan, r)

@@ -1,36 +1,42 @@
 from concourse.bass import DstId, RemoteDMATransfer
+from concourse.mybir import AluOpType, ActivationFunctionType
 
 P = 128
 R = 64
+H = P // 2
 BF = "bfloat16"
 
 SCRATCH = {
     "dm": ("dram", [P, P], BF),
     "kd": ("dram", [2, P, P], BF),
     "rd": ("dram", [P, P], BF),
-    "z": ("sbuf", [P, P + 1], BF),
-    "dz": ("dram", [P + 1, P], BF),
+    "ib": ("sbuf", [P, H], BF),
+    "on": ("sbuf", [P, H], BF),
     "w0": ("sbuf", [P, P], BF),
     "w1": ("sbuf", [P, P], BF),
     "w2": ("sbuf", [P, P], BF),
     "w3": ("sbuf", [P, P], BF),
     "w4": ("sbuf", [P, P], BF),
     "qi": ("sbuf", [P, R + P], BF),
-    "ps": ("sbuf", [P, R + P], BF),
+    "sb": ("sbuf", [P, P], BF),
+    "pb": ("sbuf", [P, R], BF),
     "o2": ("sbuf", [P, R], BF),
-    "acc": ("psum", [P, 512], "float32"),
+    "accs": ("psum", [P, 512], "float32"),
+    "accp": ("psum", [P, 512], "float32"),
     "acc2": ("psum", [P, 512], "float32"),
 }
-SEMAPHORES = ["ld_dm", "ld_w0", "ld_q", "ld_w1", "st_p", "st_q2", "fill", "seed", "idn", "in1", "cab", "xa", "xb",
-              "sent", "mm1", "cp1", "mm2", "cp2"]
+SEMAPHORES = ["ld_dm", "ld_w0", "ld_q", "ld_w1", "st_p", "st_q2", "fill", "seed", "sel", "idn", "in1", "cab", "xa", "xb",
+              "sent", "mms", "mmp", "cps", "cpp", "mm2", "cp2"]
+
+BLOCK = {"far": (0, H // 2), "near": (H // 2, H // 2), "third": (H, H)}
 
 
 def _engines(mask):
     return [e for e in range(mask.bit_length()) if (mask >> e) & 1]
 
 
-def _bits(engines):
-    return sum(1 << e for e in engines)
+def _count(mask):
+    return len(_engines(mask))
 
 
 def _plan(T, topo):
@@ -44,8 +50,9 @@ def _plan(T, topo):
         cross = [s for s in ranks if s != r and topo.host(s) == topo.host(r)][0]
         chip = [c for c in range(max(0, r - n), r + n + 1)
                 if topo.host(c) == topo.host(r) and topo.chip(c) == topo.chip(r)]
-        helper = [c for c in chip if c != r and topo.die(c) == topo.die(r) and topo.may_write(c, cross)][0]
-        plan[r] = {"partner": partner, "cabled": cabled, "cross": cross, "helper": helper}
+        ports = [c for c in chip if c != r and topo.die(c) == topo.die(r) and topo.may_write(c, cross)]
+        third = [c for c in chip if c != r and topo.die(c) == topo.die(r) and c not in ports[0:2]][0]
+        plan[r] = {"partner": partner, "cabled": cabled, "cross": cross, "far": ports[0], "near": ports[1], "third": third}
     return plan
 
 
@@ -54,102 +61,131 @@ def _dst(topo, dst, src):
     return DstId(rid=rid, pnc=pid)
 
 
-def _step1_engines(topo, plan, r):
-    mask = topo.mask(r, plan[plan[r]["partner"]]["helper"]) & topo.mask(r, plan[r]["helper"]) & topo.mask(r, plan[r]["partner"])
-    return _engines(mask)
+def _step1_masks(topo, plan, r):
+    p = plan[r]["partner"]
+    off = topo.mask(r, plan[p]["far"]) & topo.mask(r, plan[p]["near"]) & topo.mask(r, p)
+    on = topo.mask(r, plan[r]["far"]) & topo.mask(r, plan[r]["near"]) & ~off
+    return off, on
 
 
-def _helper_program(g, core, T, topo, plan, r):
+def _identity_block(g, core, T, topo, r, role, mask):
     S = T.sem
-    near = plan[r]["cross"]
-    far = plan[plan[r]["cabled"]]["cross"]
-    eng = _engines(topo.mask(core, near) & topo.mask(core, far) & topo.mask(core, r))
-    half = len(eng) // 2
-
-    g.vector.memset(T.z[:, :], 0.0).then_inc(S.fill, 1)
-    g.vector.wait_ge(S.fill, 1)
-    g.vector.memset(T.z[:, 0:1], 1.0).then_inc(S.fill, 1)
-    g.sync.wait_ge(S.fill, 2)
-    g.sync.dma_start(T.dz[:, :], T.z[:, :]).then_inc(S.seed, 16)
-    g.wait_ge(S.seed, 16)
+    first, width = BLOCK[role]
+    g.affine_select(out=T.ib[:, 0:width], in_=T.ib[:, 0:width], pattern=[[-1, width]], compare_op=AluOpType.is_equal,
+                    fill=0.0, base=-first, channel_multiplier=1).then_inc(S.sel, 1)
+    g.wait_ge(S.sel, 1)
     rid, pid = topo.addr(r, core)
-    g.remote_dma(out_ap=T.qi[:, R:R + P], in_ap=T.dz[0:P, :], remote_sem=S.idn, local_sem=S.sent,
-                 pid=pid, routing_id=rid, dma_engine_mask=_bits(eng))
+    g.remote_dma(out_ap=T.qi[:, R + first:R + first + width], in_ap=T.ib[:, 0:width], remote_sem=S.idn, local_sem=S.sent,
+                 pid=pid, routing_id=rid, dma_engine_mask=mask)
 
-    g.wait_ge(S.in1, len(_step1_engines(topo, plan, r)) + len(_step1_engines(topo, plan, plan[r]["partner"])))
-    srcs = [T.kd[0], T.kd[1]]
+
+def _third_program(g, core, T, topo, plan, r):
+    S = T.sem
+    g.wait_ge(S.seed, _count(topo.mask(r, core)))
+    _identity_block(g, core, T, topo, r, "third", topo.mask(core, r))
+    g.wait_ge(S.sent, _count(topo.mask(core, r)))
+
+
+def _helper_target(plan, r, role):
+    return plan[plan[r]["cabled"]]["cross"] if role == "far" else plan[r]["cross"]
+
+
+def _helper_mask(topo, plan, r, role):
+    k = plan[r][role]
+    return topo.mask(k, _helper_target(plan, r, role)) & topo.mask(k, r)
+
+
+def _helper_program(g, core, T, topo, plan, r, role):
+    S = T.sem
+    target = _helper_target(plan, r, role)
+    mask = _helper_mask(topo, plan, r, role)
+
+    g.vector.memset(T.ib[:, :], 1.0).then_inc(S.fill, 1)
+    g.wait_ge(S.fill, 1)
+    _identity_block(g, core, T, topo, r, role, mask)
+
+    g.wait_ge(S.in1, _count(_step1_masks(topo, plan, r)[1]) + _count(_step1_masks(topo, plan, plan[r]["partner"])[0]))
     g.remote_dma_fused([
-        RemoteDMATransfer(dst_ids=[_dst(topo, far, core)], dma_engine_mask=_bits(eng[:half]), remote_sem=S.xb,
-                          srcs=srcs, dsts=[T.w4[:, :]], alu_op=1),
-        RemoteDMATransfer(dst_ids=[_dst(topo, near, core)], dma_engine_mask=_bits(eng[half:]), remote_sem=S.xa,
-                          srcs=srcs, dsts=[T.w3[:, :]], alu_op=1),
+        RemoteDMATransfer(dst_ids=[_dst(topo, target, core)], dma_engine_mask=mask,
+                          remote_sem=S.xb if role == "far" else S.xa,
+                          srcs=[T.kd[0], T.kd[1]], dsts=[T.w4[:, :] if role == "far" else T.w3[:, :]], alu_op=1),
     ], local_sem=S.sent)
-    g.wait_ge(S.sent, 2 * len(eng))
+    g.wait_ge(S.sent, 2 * _count(mask))
 
 
 def _rank_program(g, core, T, topo, plan):
     S = T.sem
     me = plan[core]
-    partner, cabled = me["partner"], me["cabled"]
+    partner, cabled, cross = me["partner"], me["cabled"], me["cross"]
 
     g.sync.dma_start(T.dm[:, :], T.mt[:, :]).then_inc(S.ld_dm, 16)
-    g.scalar.dma_start(T.qi[:, 0:R], T.q[:, :]).then_inc(S.ld_q, 16)
-    g.scalar.dma_start(T.w0[:, :], T.mt[:, :]).then_inc(S.ld_w0, 16)
+    g.sync.dma_start(T.qi[:, 0:R], T.q[:, :]).then_inc(S.ld_q, 16)
+    g.sync.dma_start(T.w0[:, :], T.mt[:, :]).then_inc(S.ld_w0, 16)
 
-    eng1 = _step1_engines(topo, plan, core)
+    m0 = topo.mask(core, me["third"])
+    g.vector.memset(T.on[:, :], 1.0).then_inc(S.fill, 1)
+    g.wait_ge(S.fill, 1)
+    rid, pid = topo.addr(me["third"], core)
+    g.remote_dma(out_ap=T.ib[:, :], in_ap=T.on[:, :], remote_sem=S.seed, local_sem=S.sent,
+                 pid=pid, routing_id=rid, dma_engine_mask=m0)
+
+    off, on = _step1_masks(topo, plan, core)
     g.wait_ge(S.ld_dm, 16)
     g.remote_dma_fused([
-        RemoteDMATransfer(dst_ids=[_dst(topo, plan[partner]["helper"], core), _dst(topo, me["helper"], core),
+        RemoteDMATransfer(dst_ids=[_dst(topo, plan[partner]["far"], core), _dst(topo, plan[partner]["near"], core),
                                    _dst(topo, partner, core)],
-                          dma_engine_mask=_bits(eng1), remote_sem=S.in1,
-                          srcs=[T.dm[:, :]], dsts=[T.kd[1], T.kd[0], T.rd[:, :]], alu_op=0),
+                          dma_engine_mask=off, remote_sem=S.in1,
+                          srcs=[T.dm[:, :]], dsts=[T.kd[1], T.kd[1], T.rd[:, :]], alu_op=0),
+        RemoteDMATransfer(dst_ids=[_dst(topo, me["far"], core), _dst(topo, me["near"], core)],
+                          dma_engine_mask=on, remote_sem=S.in1,
+                          srcs=[T.dm[:, :]], dsts=[T.kd[0], T.kd[0]], alu_op=0),
     ], local_sem=S.sent)
 
-    n_in = len(_step1_engines(topo, plan, partner))
-    eng2 = _engines(topo.mask(core, cabled))
+    n_in = _count(_step1_masks(topo, plan, partner)[0])
+    m2 = topo.mask(core, cabled)
     g.wait_ge(S.in1, n_in)
     g.remote_dma_fused([
-        RemoteDMATransfer(dst_ids=[_dst(topo, cabled, core)], dma_engine_mask=_bits(eng2), remote_sem=S.cab,
+        RemoteDMATransfer(dst_ids=[_dst(topo, cabled, core)], dma_engine_mask=m2, remote_sem=S.cab,
                           srcs=[T.dm[:, :], T.rd[:, :]], dsts=[T.w2[:, :]], alu_op=1),
     ], local_sem=S.sent)
     g.sync.wait_ge(S.in1, n_in)
     g.sync.dma_start(T.w1[:, :], T.rd[:, :]).then_inc(S.ld_w1, 16)
 
-    def helper_engines(r):
-        k = plan[r]["helper"]
-        return _engines(topo.mask(k, plan[r]["cross"]) & topo.mask(k, plan[plan[r]["cabled"]]["cross"]) & topo.mask(k, r))
-
-    n_idn = len(helper_engines(core))
-    n_xa = len(helper_engines(me["cross"])) - len(helper_engines(me["cross"])) // 2
-    n_xb = len(helper_engines(plan[cabled]["cross"])) // 2
-    n_cab = len(_engines(topo.mask(cabled, core)))
-    t, v = g.tensor, g.vector
-    out1 = T.acc[:, 0:R + P]
+    n_idn = (_count(_helper_mask(topo, plan, core, "far")) + _count(_helper_mask(topo, plan, core, "near"))
+             + _count(topo.mask(me["third"], core)))
+    n_xa = _count(_helper_mask(topo, plan, cross, "near"))
+    n_xb = _count(_helper_mask(topo, plan, plan[cross]["cabled"], "far"))
+    n_cab = _count(topo.mask(cabled, core))
+    t, v, a = g.tensor, g.vector, g.scalar
+    outs, outp = T.accs[:, 0:P], T.accp[:, 0:R]
+    eye, q = T.qi[:, R:R + P], T.qi[:, 0:R]
     t.wait_ge(S.ld_q, 16)
     t.wait_ge(S.idn, n_idn)
-    t.wait_ge(S.ld_w0, 16)
-    t.matmul(out1, T.w0[:, :], T.qi[:, :], True, False)
-    t.wait_ge(S.ld_w1, 16)
-    t.matmul(out1, T.w1[:, :], T.qi[:, :], False, False)
-    t.wait_ge(S.cab, n_cab)
-    t.matmul(out1, T.w2[:, :], T.qi[:, :], False, False)
-    t.wait_ge(S.xa, n_xa)
-    t.matmul(out1, T.w3[:, :], T.qi[:, :], False, False)
-    t.wait_ge(S.xb, n_xb)
-    t.matmul(out1, T.w4[:, :], T.qi[:, :], False, True).then_inc(S.mm1, 1)
-    v.wait_ge(S.mm1, 1)
-    v.tensor_copy(T.ps[:, :], out1).then_inc(S.cp1, 1)
-    g.scalar.wait_ge(S.cp1, 1)
-    g.scalar.dma_start(T.p[:, :], T.ps[:, 0:R]).then_inc(S.st_p, 16)
-    t.wait_ge(S.cp1, 1)
-    t.matmul(T.acc2[:, 0:R], T.ps[:, R:R + P], T.ps[:, 0:R], True, True).then_inc(S.mm2, 1)
+    slots = [(T.w0, S.ld_w0, 16), (T.w1, S.ld_w1, 16), (T.w3, S.xa, n_xa), (T.w4, S.xb, n_xb), (T.w2, S.cab, n_cab)]
+    for i, (w, sem, n) in enumerate(slots):
+        first, last = i == 0, i == len(slots) - 1
+        t.wait_ge(sem, n)
+        ms = t.matmul(outs, w[:, :], eye, first, last)
+        mp = t.matmul(outp, w[:, :], q, first, last)
+        if last:
+            ms.then_inc(S.mms, 1)
+            mp.then_inc(S.mmp, 1)
+    v.wait_ge(S.mms, 1)
+    v.tensor_copy(T.sb[:, :], outs).then_inc(S.cps, 1)
+    a.wait_ge(S.mmp, 1)
+    a.activation(T.pb[:, :], outp, ActivationFunctionType.Copy).then_inc(S.cpp, 1)
+    a.wait_ge(S.cpp, 1)
+    a.dma_start(T.p[:, :], T.pb[:, :]).then_inc(S.st_p, 16)
+    t.wait_ge(S.cps, 1)
+    t.wait_ge(S.cpp, 1)
+    t.matmul(T.acc2[:, 0:R], T.sb[:, :], T.pb[:, :], True, True).then_inc(S.mm2, 1)
     v.wait_ge(S.mm2, 1)
     v.tensor_copy(T.o2[:, :], T.acc2[:, 0:R]).then_inc(S.cp2, 1)
     g.sync.wait_ge(S.cp2, 1)
     g.sync.dma_start(T.q2[:, :], T.o2[:, :]).then_inc(S.st_q2, 16)
 
-    g.wait_ge(S.sent, len(eng1) + len(eng2))
-    g.scalar.wait_ge(S.st_p, 16)
+    g.wait_ge(S.sent, _count(m0) + _count(off) + _count(on) + _count(m2))
+    a.wait_ge(S.st_p, 16)
     g.sync.wait_ge(S.st_q2, 16)
 
 
@@ -159,5 +195,8 @@ def rank_program(g, core, T, topo):
         _rank_program(g, core, T, topo, plan)
         return
     for r in plan:
-        if plan[r]["helper"] == core:
-            _helper_program(g, core, T, topo, plan, r)
+        for role in ("far", "near"):
+            if plan[r][role] == core:
+                _helper_program(g, core, T, topo, plan, r, role)
+        if plan[r]["third"] == core:
+            _third_program(g, core, T, topo, plan, r)

from concourse.bass import DstId, RemoteDMATransfer
from concourse.mybir import AluOpType, ActivationFunctionType

P = 128
R = 64
H = P // 2
BF = "bfloat16"

SCRATCH = {
    "dm": ("dram", [P, P], BF),
    "kd": ("dram", [2, P, P], BF),
    "rd": ("dram", [P, P], BF),
    "ib": ("sbuf", [P, H], BF),
    "on": ("sbuf", [P, H], BF),
    "w0": ("sbuf", [P, P], BF),
    "w1": ("sbuf", [P, P], BF),
    "w2": ("sbuf", [P, P], BF),
    "w3": ("sbuf", [P, P], BF),
    "w4": ("sbuf", [P, P], BF),
    "qi": ("sbuf", [P, R + P], BF),
    "sb": ("sbuf", [P, P], BF),
    "pb": ("sbuf", [P, R], BF),
    "o2": ("sbuf", [P, R], BF),
    "accs": ("psum", [P, 512], "float32"),
    "accp": ("psum", [P, 512], "float32"),
    "acc2": ("psum", [P, 512], "float32"),
}
SEMAPHORES = ["ld_dm", "ld_w0", "ld_q", "ld_w1", "st_p", "st_q2", "fill", "seed", "sel", "idn", "in1", "cab", "xa", "xb",
              "sent", "mms", "mmp", "cps", "cpp", "mm2", "cp2"]

BLOCK = {"far": (0, H // 2), "near": (H // 2, H // 2), "third": (H, H)}


def _engines(mask):
    return [e for e in range(mask.bit_length()) if (mask >> e) & 1]


def _count(mask):
    return len(_engines(mask))


def _plan(T, topo):
    ranks = list(T.cores)
    n = topo.CORES_PER_CHIP
    plan = {}
    for r in ranks:
        partner = [s for s in ranks if topo.same_plane(r, s)][0]
        cabled = [s for s in ranks if topo.rack(topo.host(s)) != topo.rack(topo.host(r))
                  and topo.chip(s) == topo.chip(r) and topo.may_write(r, s)][0]
        cross = [s for s in ranks if s != r and topo.host(s) == topo.host(r)][0]
        chip = [c for c in range(max(0, r - n), r + n + 1)
                if topo.host(c) == topo.host(r) and topo.chip(c) == topo.chip(r)]
        ports = [c for c in chip if c != r and topo.die(c) == topo.die(r) and topo.may_write(c, cross)]
        third = [c for c in chip if c != r and topo.die(c) == topo.die(r) and c not in ports[0:2]][0]
        plan[r] = {"partner": partner, "cabled": cabled, "cross": cross, "far": ports[0], "near": ports[1], "third": third}
    return plan


def _dst(topo, dst, src):
    rid, pid = topo.addr(dst, src)
    return DstId(rid=rid, pnc=pid)


def _step1_masks(topo, plan, r):
    p = plan[r]["partner"]
    off = topo.mask(r, plan[p]["far"]) & topo.mask(r, plan[p]["near"]) & topo.mask(r, p)
    on = topo.mask(r, plan[r]["far"]) & topo.mask(r, plan[r]["near"]) & ~off
    return off, on


def _identity_block(g, core, T, topo, r, role, mask):
    S = T.sem
    first, width = BLOCK[role]
    g.affine_select(out=T.ib[:, 0:width], in_=T.ib[:, 0:width], pattern=[[-1, width]], compare_op=AluOpType.is_equal,
                    fill=0.0, base=-first, channel_multiplier=1).then_inc(S.sel, 1)
    g.wait_ge(S.sel, 1)
    rid, pid = topo.addr(r, core)
    g.remote_dma(out_ap=T.qi[:, R + first:R + first + width], in_ap=T.ib[:, 0:width], remote_sem=S.idn, local_sem=S.sent,
                 pid=pid, routing_id=rid, dma_engine_mask=mask)


def _third_program(g, core, T, topo, plan, r):
    S = T.sem
    g.wait_ge(S.seed, _count(topo.mask(r, core)))
    _identity_block(g, core, T, topo, r, "third", topo.mask(core, r))
    g.wait_ge(S.sent, _count(topo.mask(core, r)))


def _helper_target(plan, r, role):
    return plan[plan[r]["cabled"]]["cross"] if role == "far" else plan[r]["cross"]


def _helper_mask(topo, plan, r, role):
    k = plan[r][role]
    return topo.mask(k, _helper_target(plan, r, role)) & topo.mask(k, r)


def _helper_program(g, core, T, topo, plan, r, role):
    S = T.sem
    target = _helper_target(plan, r, role)
    mask = _helper_mask(topo, plan, r, role)

    g.vector.memset(T.ib[:, :], 1.0).then_inc(S.fill, 1)
    g.wait_ge(S.fill, 1)
    _identity_block(g, core, T, topo, r, role, mask)

    g.wait_ge(S.in1, _count(_step1_masks(topo, plan, r)[1]) + _count(_step1_masks(topo, plan, plan[r]["partner"])[0]))
    g.remote_dma_fused([
        RemoteDMATransfer(dst_ids=[_dst(topo, target, core)], dma_engine_mask=mask,
                          remote_sem=S.xb if role == "far" else S.xa,
                          srcs=[T.kd[0], T.kd[1]], dsts=[T.w4[:, :] if role == "far" else T.w3[:, :]], alu_op=1),
    ], local_sem=S.sent)
    g.wait_ge(S.sent, 2 * _count(mask))


def _rank_program(g, core, T, topo, plan):
    S = T.sem
    me = plan[core]
    partner, cabled, cross = me["partner"], me["cabled"], me["cross"]

    g.sync.dma_start(T.dm[:, :], T.mt[:, :]).then_inc(S.ld_dm, 16)
    g.sync.dma_start(T.qi[:, 0:R], T.q[:, :]).then_inc(S.ld_q, 16)
    g.sync.dma_start(T.w0[:, :], T.mt[:, :]).then_inc(S.ld_w0, 16)

    m0 = topo.mask(core, me["third"])
    g.vector.memset(T.on[:, :], 1.0).then_inc(S.fill, 1)
    g.wait_ge(S.fill, 1)
    rid, pid = topo.addr(me["third"], core)
    g.remote_dma(out_ap=T.ib[:, :], in_ap=T.on[:, :], remote_sem=S.seed, local_sem=S.sent,
                 pid=pid, routing_id=rid, dma_engine_mask=m0)

    off, on = _step1_masks(topo, plan, core)
    g.wait_ge(S.ld_dm, 16)
    g.remote_dma_fused([
        RemoteDMATransfer(dst_ids=[_dst(topo, plan[partner]["far"], core), _dst(topo, plan[partner]["near"], core),
                                   _dst(topo, partner, core)],
                          dma_engine_mask=off, remote_sem=S.in1,
                          srcs=[T.dm[:, :]], dsts=[T.kd[1], T.kd[1], T.rd[:, :]], alu_op=0),
        RemoteDMATransfer(dst_ids=[_dst(topo, me["far"], core), _dst(topo, me["near"], core)],
                          dma_engine_mask=on, remote_sem=S.in1,
                          srcs=[T.dm[:, :]], dsts=[T.kd[0], T.kd[0]], alu_op=0),
    ], local_sem=S.sent)

    n_in = _count(_step1_masks(topo, plan, partner)[0])
    m2 = topo.mask(core, cabled)
    g.wait_ge(S.in1, n_in)
    g.remote_dma_fused([
        RemoteDMATransfer(dst_ids=[_dst(topo, cabled, core)], dma_engine_mask=m2, remote_sem=S.cab,
                          srcs=[T.dm[:, :], T.rd[:, :]], dsts=[T.w2[:, :]], alu_op=1),
    ], local_sem=S.sent)
    g.sync.wait_ge(S.in1, n_in)
    g.sync.dma_start(T.w1[:, :], T.rd[:, :]).then_inc(S.ld_w1, 16)

    n_idn = (_count(_helper_mask(topo, plan, core, "far")) + _count(_helper_mask(topo, plan, core, "near"))
             + _count(topo.mask(me["third"], core)))
    n_xa = _count(_helper_mask(topo, plan, cross, "near"))
    n_xb = _count(_helper_mask(topo, plan, plan[cross]["cabled"], "far"))
    n_cab = _count(topo.mask(cabled, core))
    t, v, a = g.tensor, g.vector, g.scalar
    outs, outp = T.accs[:, 0:P], T.accp[:, 0:R]
    eye, q = T.qi[:, R:R + P], T.qi[:, 0:R]
    t.wait_ge(S.ld_q, 16)
    t.wait_ge(S.idn, n_idn)
    slots = [(T.w0, S.ld_w0, 16), (T.w1, S.ld_w1, 16), (T.w3, S.xa, n_xa), (T.w4, S.xb, n_xb), (T.w2, S.cab, n_cab)]
    for i, (w, sem, n) in enumerate(slots):
        first, last = i == 0, i == len(slots) - 1
        t.wait_ge(sem, n)
        ms = t.matmul(outs, w[:, :], eye, first, last)
        mp = t.matmul(outp, w[:, :], q, first, last)
        if last:
            ms.then_inc(S.mms, 1)
            mp.then_inc(S.mmp, 1)
    v.wait_ge(S.mms, 1)
    v.tensor_copy(T.sb[:, :], outs).then_inc(S.cps, 1)
    a.wait_ge(S.mmp, 1)
    a.activation(T.pb[:, :], outp, ActivationFunctionType.Copy).then_inc(S.cpp, 1)
    a.wait_ge(S.cpp, 1)
    a.dma_start(T.p[:, :], T.pb[:, :]).then_inc(S.st_p, 16)
    t.wait_ge(S.cps, 1)
    t.wait_ge(S.cpp, 1)
    t.matmul(T.acc2[:, 0:R], T.sb[:, :], T.pb[:, :], True, True).then_inc(S.mm2, 1)
    v.wait_ge(S.mm2, 1)
    v.tensor_copy(T.o2[:, :], T.acc2[:, 0:R]).then_inc(S.cp2, 1)
    g.sync.wait_ge(S.cp2, 1)
    g.sync.dma_start(T.q2[:, :], T.o2[:, :]).then_inc(S.st_q2, 16)

    g.wait_ge(S.sent, _count(m0) + _count(off) + _count(on) + _count(m2))
    a.wait_ge(S.st_p, 16)
    g.sync.wait_ge(S.st_q2, 16)


def rank_program(g, core, T, topo):
    plan = _plan(T, topo)
    if T.rank_of(core) is not None:
        _rank_program(g, core, T, topo, plan)
        return
    for r in plan:
        for role in ("far", "near"):
            if plan[r][role] == core:
                _helper_program(g, core, T, topo, plan, r, role)
        if plan[r]["third"] == core:
            _third_program(g, core, T, topo, plan, r)
